import numpy as np, ml_dtypes
CORES = [5,21,45,77,85,101,109,125,133,141,189,213]
N = 12
TK = 256
COEF = [[-1,2,-2,-2,3,-2,3,-2,-2,-1,1,2],[3,-2,-1,-1,-1,3,2,1,2,2,-2,3],[1,2,-1,-1,-1,-2,-1,2,1,2,1,-2],[-1,2,-1,-1,-2,-2,2,3,3,-1,-1,-2],[2,-2,-2,1,1,1,-1,2,1,-1,-2,-1],[2,3,-2,3,-1,2,1,-2,2,-2,2,3],[1,1,-2,3,1,2,3,-2,-1,2,-1,-1],[1,3,-1,1,-1,3,-1,1,3,2,-2,2],[1,1,-1,-1,-1,1,2,-2,3,-2,3,-2],[-1,1,-2,1,-1,2,1,2,3,3,3,2],[3,2,1,-1,1,1,1,-1,3,-1,2,-2],[-2,-2,-2,1,1,1,2,3,-2,1,-2,3]]
def setup_inputs(rng):
    return {"x": rng.standard_normal((N, 128, TK), dtype=np.float32).astype(ml_dtypes.bfloat16), "a": (rng.standard_normal((N, 128, 128), dtype=np.float32) / 11).astype(ml_dtypes.bfloat16)}
def setup_inputs_big(rng):
    d = setup_inputs(rng)
    for k in ("x", "a"): d[k] = (d[k].astype(np.float32) * 1024.0).astype(d[k].dtype)
    return d
def setup_inputs_small(rng):
    d = setup_inputs(rng)
    for k in ("x", "a"): d[k] = (d[k].astype(np.float32) * (1 / 1024.0)).astype(d[k].dtype)
    return d
def setup_inputs_apart(rng):
    d = setup_inputs(rng)
    f = (10.0 ** rng.permutation(np.linspace(-1.5, 1.5, N))).astype(np.float32).reshape(N, 1, 1)
    for k in ("x", "a"): d[k] = (d[k].astype(np.float32) * f).astype(d[k].dtype)
    return d
def reference(x, a):
    X, A = x.astype(np.float64), a.astype(np.float64)
    y = np.stack([A[r].T @ sum(COEF[r][j] * X[j] for j in range(N)) for r in range(N)])
    return {"y": y.astype(ml_dtypes.bfloat16)}

@@ -1,0 +1,131 @@
+from concourse.bass import DstId, RemoteDMATransfer
+from concourse.mybir import AluOpType
+
+N = 12
+TK = 256
+M = 128
+NSIM = 256
+SCALES = (1, 2, -1, 3, -2)
+SHARES = ((False, 3, 8), (False, 2, 8), (True, 1, 8))
+N_ON = 8
+N_DIRECT = 8
+
+SCRATCH = {
+    "xg": ("sbuf", [128, N * TK], "bfloat16"),
+    "av": ("sbuf", [128, len(SCALES) * M], "bfloat16"),
+    "ys": ("sbuf", [128, TK], "bfloat16"),
+    "acc": ("psum", [128, TK], "float32"),
+}
+SEMAPHORES = ["ldx", "lda", "sc", "mm", "cp", "st", "sent"] + ["arr%d" % j for j in range(N)]
+
+
+def _bits(m):
+    return [b for b in range(m.bit_length()) if (m >> b) & 1]
+
+
+def _mask(bits):
+    m = 0
+    for b in bits:
+        m |= 1 << b
+    return m
+
+
+def _plan(cores, topo):
+    planes = []
+    for r in range(len(cores)):
+        for p in planes:
+            if topo.same_plane(cores[p[0]], cores[r]):
+                p.append(r)
+                break
+        else:
+            planes.append([r])
+    plan = []
+    for j, me in enumerate(cores):
+        own = [p for p in planes if j in p][0]
+        s = own.index(j)
+        direct = [own[(s + k) % len(own)] for k in range(1, len(own))]
+        cross = []
+        for p in planes:
+            if p is not own:
+                cross += [p[(s + k) % len(p)] for k in range(len(p))]
+        onchip = [c for c in range(NSIM) if c != me and topo.host(c) == topo.host(me) and topo.chip(c) == topo.chip(me)]
+        able = [c for c in onchip if all(topo.may_write(c, cores[d]) for d in cross)]
+        near = [c for c in able if topo.die(c) == topo.die(me)]
+        far = [c for c in able if topo.die(c) != topo.die(me)]
+        relays, at = [], 0
+        for same_die, cnt, eng in SHARES:
+            c = (near if same_die else far).pop(0)
+            relays.append((c, cross[at:at + cnt], eng))
+            at += cnt
+        plan.append({"direct": direct, "relays": relays})
+    return plan
+
+
+def _send(g, T, topo, core, cores, j, dests, bits, local_sem):
+    slot = T.xg[:, j * TK:(j + 1) * TK]
+    ids = []
+    for d in dests:
+        rid, pid = topo.addr(d, core)
+        ids.append(DstId(rid=rid, pnc=pid))
+    g.remote_dma_fused([RemoteDMATransfer(dst_ids=ids, dma_engine_mask=_mask(bits), remote_sem=T.sem["arr%d" % j],
+                                          srcs=[slot], dsts=[slot] * len(dests), alu_op=0)], local_sem=local_sem)
+
+
+def rank_program(g, core, T, topo):
+    cores = list(T.cores)
+    plan = _plan(cores, topo)
+    rank = T.rank_of(core)
+
+    if rank is None:
+        for j, pl in enumerate(plan):
+            for c, dests, eng in pl["relays"]:
+                if c == core:
+                    bits = _bits(topo.mask(core, cores[dests[0]]))[:eng]
+                    g.wait_ge(T.sem["arr%d" % j], N_ON)
+                    _send(g, T, topo, core, cores, j, [cores[d] for d in dests], bits, T.sem.sent)
+                    g.wait_ge(T.sem.sent, eng)
+        return
+
+    pl = plan[rank]
+    coef = T.tables["COEF"][rank]
+    av = [T.av[:, k * M:(k + 1) * M] for k in range(len(SCALES))]
+
+    g.sync.dma_start(T.xg[:, rank * TK:(rank + 1) * TK], T.x[:]).then_inc(T.sem.ldx, 16)
+    g.sync.dma_start(av[0], T.a[:]).then_inc(T.sem.lda, 16)
+
+    off = _bits(topo.mask(core, cores[pl["direct"][0]]))
+    on_only = [b for b in _bits(topo.mask(core, pl["relays"][0][0])) if b not in off]
+    g.wait_ge(T.sem.ldx, 16)
+    _send(g, T, topo, core, cores, rank, [c for c, _, _ in pl["relays"]], on_only[:N_ON], T.sem.sent)
+    _send(g, T, topo, core, cores, rank, [cores[d] for d in pl["direct"]], off[:N_DIRECT], T.sem.sent)
+
+    v = g.vector
+    v.wait_ge(T.sem.lda, 16)
+    v.tensor_tensor(av[1], av[0], av[0], AluOpType.add).then_inc(T.sem.sc, 1)
+    v.wait_ge(T.sem.sc, 1)
+    v.tensor_tensor(av[2], av[0], av[1], AluOpType.subtract).then_inc(T.sem.sc, 1)
+    v.tensor_tensor(av[3], av[1], av[0], AluOpType.add).then_inc(T.sem.sc, 1)
+    v.wait_ge(T.sem.sc, 3)
+    v.tensor_tensor(av[4], av[2], av[0], AluOpType.subtract).then_inc(T.sem.sc, 1)
+
+    due = [(-1.0, rank, T.sem.ldx, 16)]
+    for j, p in enumerate(plan):
+        if rank in p["direct"]:
+            due.append((p["direct"].index(rank) + 1.0, j, T.sem["arr%d" % j], N_DIRECT))
+        for k, (c, dests, eng) in enumerate(p["relays"]):
+            if rank in dests:
+                due.append((100.0 + k + 1 + dests.index(rank) + 1, j, T.sem["arr%d" % j], eng))
+    due.sort(key=lambda t: (t[0], t[1]))
+    te = g.tensor
+    te.wait_ge(T.sem.sc, 4)
+    for i, (_, j, sem, cnt) in enumerate(due):
+        te.wait_ge(sem, cnt)
+        mmi = te.matmul(T.acc[:], av[SCALES.index(coef[j])], T.xg[:, j * TK:(j + 1) * TK], start=(i == 0), stop=(i == N - 1))
+    mmi.then_inc(T.sem.mm, 1)
+
+    v.wait_ge(T.sem.mm, 1)
+    v.tensor_copy(T.ys[:], T.acc[:]).then_inc(T.sem.cp, 1)
+    g.sync.wait_ge(T.sem.cp, 1)
+    g.sync.dma_start(T.y[:], T.ys[:]).then_inc(T.sem.st, 16)
+    g.sync.wait_ge(T.sem.st, 16)
+    g.wait_ge(T.sem.sent, N_ON + N_DIRECT)

@@ -6,17 +6,20 @@ TK = 256
 M = 128
 NSIM = 256
 SCALES = (1, 2, -1, 3, -2)
-SHARES = ((False, 3, 8), (False, 2, 8), (True, 1, 8))
+N_OWN = 3
+HELPERS = ((True, False, 2), (True, True, 2), (True, False, 1), (True, True, 1), (False, False, 1), (False, False, 1))
 N_ON = 8
-N_DIRECT = 8
+N_OFF = 8
 
 SCRATCH = {
+    "xd": ("dram", [128, TK], "bfloat16"),
     "xg": ("sbuf", [128, N * TK], "bfloat16"),
     "av": ("sbuf", [128, len(SCALES) * M], "bfloat16"),
     "ys": ("sbuf", [128, TK], "bfloat16"),
-    "acc": ("psum", [128, TK], "float32"),
+    "acc0": ("psum", [128, 512], "float32"),
+    "acc1": ("psum", [128, 512], "float32"),
 }
-SEMAPHORES = ["ldx", "lda", "sc", "mm", "cp", "st", "sent"] + ["arr%d" % j for j in range(N)]
+SEMAPHORES = ["ldd", "ldx", "lda", "sc", "mm0", "mm1", "cp", "st", "sent", "gone"] + ["arr%d" % j for j in range(N)]
 
 
 def _bits(m):
@@ -43,32 +46,35 @@ def _plan(cores, topo):
     for j, me in enumerate(cores):
         own = [p for p in planes if j in p][0]
         s = own.index(j)
-        direct = [own[(s + k) % len(own)] for k in range(1, len(own))]
+        inpl = [own[(s + k) % len(own)] for k in range(1, len(own))]
         cross = []
         for p in planes:
             if p is not own:
                 cross += [p[(s + k) % len(p)] for k in range(len(p))]
         onchip = [c for c in range(NSIM) if c != me and topo.host(c) == topo.host(me) and topo.chip(c) == topo.chip(me)]
         able = [c for c in onchip if all(topo.may_write(c, cores[d]) for d in cross)]
-        near = [c for c in able if topo.die(c) == topo.die(me)]
-        far = [c for c in able if topo.die(c) != topo.die(me)]
-        relays, at = [], 0
-        for same_die, cnt, eng in SHARES:
-            c = (near if same_die else far).pop(0)
-            relays.append((c, cross[at:at + cnt], eng))
-            at += cnt
-        plan.append({"direct": direct, "relays": relays})
+        plain = [c for c in onchip if c not in able and all(topo.may_write(c, cores[d]) for d in inpl)]
+        pools = {}
+        for x_plane, pool in ((True, able), (False, plain)):
+            pools[(x_plane, True)] = [c for c in pool if topo.die(c) == topo.die(me)]
+            pools[(x_plane, False)] = [c for c in pool if topo.die(c) != topo.die(me)]
+        left = {True: list(cross), False: inpl[N_OWN:]}
+        helpers = []
+        for x_plane, same_die, cnt in HELPERS:
+            c = pools[(x_plane, same_die)].pop(0)
+            helpers.append((c, left[x_plane][:cnt]))
+            left[x_plane] = left[x_plane][cnt:]
+        plan.append({"direct": inpl[:N_OWN], "helpers": helpers})
     return plan
 
 
-def _send(g, T, topo, core, cores, j, dests, bits, local_sem):
-    slot = T.xg[:, j * TK:(j + 1) * TK]
+def _send(g, T, topo, core, dests, src, dst, bits, sem, local_sem):
     ids = []
     for d in dests:
         rid, pid = topo.addr(d, core)
         ids.append(DstId(rid=rid, pnc=pid))
-    g.remote_dma_fused([RemoteDMATransfer(dst_ids=ids, dma_engine_mask=_mask(bits), remote_sem=T.sem["arr%d" % j],
-                                          srcs=[slot], dsts=[slot] * len(dests), alu_op=0)], local_sem=local_sem)
+    g.remote_dma_fused([RemoteDMATransfer(dst_ids=ids, dma_engine_mask=_mask(bits), remote_sem=sem,
+                                          srcs=[src], dsts=[dst] * len(dests), alu_op=0)], local_sem=local_sem)
 
 
 def rank_program(g, core, T, topo):
@@ -78,26 +84,31 @@ def rank_program(g, core, T, topo):
 
     if rank is None:
         for j, pl in enumerate(plan):
-            for c, dests, eng in pl["relays"]:
+            for c, dests in pl["helpers"]:
                 if c == core:
-                    bits = _bits(topo.mask(core, cores[dests[0]]))[:eng]
+                    bits = _bits(topo.mask(core, cores[dests[0]]))[:N_OFF]
                     g.wait_ge(T.sem["arr%d" % j], N_ON)
-                    _send(g, T, topo, core, cores, j, [cores[d] for d in dests], bits, T.sem.sent)
-                    g.wait_ge(T.sem.sent, eng)
+                    _send(g, T, topo, core, [cores[d] for d in dests], T.xd[:], T.xg[:, j * TK:(j + 1) * TK], bits,
+                          T.sem["arr%d" % j], T.sem.sent)
+                    g.wait_ge(T.sem.sent, N_OFF)
         return
 
     pl = plan[rank]
     coef = T.tables["COEF"][rank]
     av = [T.av[:, k * M:(k + 1) * M] for k in range(len(SCALES))]
+    slot = T.xg[:, rank * TK:(rank + 1) * TK]
+    arr = T.sem["arr%d" % rank]
 
-    g.sync.dma_start(T.xg[:, rank * TK:(rank + 1) * TK], T.x[:]).then_inc(T.sem.ldx, 16)
+    g.sync.dma_start(T.xd[:], T.x[:]).then_inc(T.sem.ldd, 16)
     g.sync.dma_start(av[0], T.a[:]).then_inc(T.sem.lda, 16)
+    g.sync.wait_ge(T.sem.gone, N_ON)
+    g.sync.dma_start(slot, T.x[:]).then_inc(T.sem.ldx, 16)
 
     off = _bits(topo.mask(core, cores[pl["direct"][0]]))
-    on_only = [b for b in _bits(topo.mask(core, pl["relays"][0][0])) if b not in off]
-    g.wait_ge(T.sem.ldx, 16)
-    _send(g, T, topo, core, cores, rank, [c for c, _, _ in pl["relays"]], on_only[:N_ON], T.sem.sent)
-    _send(g, T, topo, core, cores, rank, [cores[d] for d in pl["direct"]], off[:N_DIRECT], T.sem.sent)
+    on_only = [b for b in _bits(topo.mask(core, pl["helpers"][0][0])) if b not in off]
+    g.wait_ge(T.sem.ldd, 16)
+    _send(g, T, topo, core, [c for c, _ in pl["helpers"]], T.xd[:], T.xd[:], on_only[:N_ON], arr, T.sem.gone)
+    _send(g, T, topo, core, [cores[d] for d in pl["direct"]], T.xd[:], slot, off[:N_OFF], arr, T.sem.sent)
 
     v = g.vector
     v.wait_ge(T.sem.lda, 16)
@@ -108,24 +119,30 @@ def rank_program(g, core, T, topo):
     v.wait_ge(T.sem.sc, 3)
     v.tensor_tensor(av[4], av[2], av[0], AluOpType.subtract).then_inc(T.sem.sc, 1)
 
-    due = [(-1.0, rank, T.sem.ldx, 16)]
+    due = [(3.5, rank, T.sem.ldx, 16)]
     for j, p in enumerate(plan):
         if rank in p["direct"]:
-            due.append((p["direct"].index(rank) + 1.0, j, T.sem["arr%d" % j], N_DIRECT))
-        for k, (c, dests, eng) in enumerate(p["relays"]):
+            due.append((p["direct"].index(rank) + 1.0, j, T.sem["arr%d" % j], N_OFF))
+        for k, (c, dests) in enumerate(p["helpers"]):
             if rank in dests:
-                due.append((100.0 + k + 1 + dests.index(rank) + 1, j, T.sem["arr%d" % j], eng))
+                due.append((1.4 + 0.4 * (k + 1) + dests.index(rank) + 1.0, j, T.sem["arr%d" % j], N_OFF))
     due.sort(key=lambda t: (t[0], t[1]))
     te = g.tensor
     te.wait_ge(T.sem.sc, 4)
+    H = TK // 2
     for i, (_, j, sem, cnt) in enumerate(due):
         te.wait_ge(sem, cnt)
-        mmi = te.matmul(T.acc[:], av[SCALES.index(coef[j])], T.xg[:, j * TK:(j + 1) * TK], start=(i == 0), stop=(i == N - 1))
-    mmi.then_inc(T.sem.mm, 1)
+        lhs = av[SCALES.index(coef[j])]
+        m0 = te.matmul(T.acc0[:, 0:H], lhs, T.xg[:, j * TK:j * TK + H], start=(i == 0), stop=(i == N - 1))
+        m1 = te.matmul(T.acc1[:, 0:H], lhs, T.xg[:, j * TK + H:(j + 1) * TK], start=(i == 0), stop=(i == N - 1))
+    m0.then_inc(T.sem.mm0, 1)
+    m1.then_inc(T.sem.mm1, 1)
 
-    v.wait_ge(T.sem.mm, 1)
-    v.tensor_copy(T.ys[:], T.acc[:]).then_inc(T.sem.cp, 1)
-    g.sync.wait_ge(T.sem.cp, 1)
+    v.wait_ge(T.sem.mm0, 1)
+    v.tensor_copy(T.ys[:, 0:H], T.acc0[:, 0:H]).then_inc(T.sem.cp, 1)
+    v.wait_ge(T.sem.mm1, 1)
+    v.tensor_copy(T.ys[:, H:TK], T.acc1[:, 0:H]).then_inc(T.sem.cp, 1)
+    g.sync.wait_ge(T.sem.cp, 2)
     g.sync.dma_start(T.y[:], T.ys[:]).then_inc(T.sem.st, 16)
     g.sync.wait_ge(T.sem.st, 16)
-    g.wait_ge(T.sem.sent, N_ON + N_DIRECT)
+    g.wait_ge(T.sem.sent, N_OFF)

from concourse.bass import DstId, RemoteDMATransfer
from concourse.mybir import AluOpType

N = 12
TK = 256
M = 128
NSIM = 256
SCALES = (1, 2, -1, 3, -2)
N_OWN = 3
HELPERS = ((True, False, 2), (True, True, 2), (True, False, 1), (True, True, 1), (False, False, 1), (False, False, 1))
N_ON = 8
N_OFF = 8

SCRATCH = {
    "xd": ("dram", [128, TK], "bfloat16"),
    "xg": ("sbuf", [128, N * TK], "bfloat16"),
    "av": ("sbuf", [128, len(SCALES) * M], "bfloat16"),
    "ys": ("sbuf", [128, TK], "bfloat16"),
    "acc0": ("psum", [128, 512], "float32"),
    "acc1": ("psum", [128, 512], "float32"),
}
SEMAPHORES = ["ldd", "ldx", "lda", "sc", "mm0", "mm1", "cp", "st", "sent", "gone"] + ["arr%d" % j for j in range(N)]


def _bits(m):
    return [b for b in range(m.bit_length()) if (m >> b) & 1]


def _mask(bits):
    m = 0
    for b in bits:
        m |= 1 << b
    return m


def _plan(cores, topo):
    planes = []
    for r in range(len(cores)):
        for p in planes:
            if topo.same_plane(cores[p[0]], cores[r]):
                p.append(r)
                break
        else:
            planes.append([r])
    plan = []
    for j, me in enumerate(cores):
        own = [p for p in planes if j in p][0]
        s = own.index(j)
        inpl = [own[(s + k) % len(own)] for k in range(1, len(own))]
        cross = []
        for p in planes:
            if p is not own:
                cross += [p[(s + k) % len(p)] for k in range(len(p))]
        onchip = [c for c in range(NSIM) if c != me and topo.host(c) == topo.host(me) and topo.chip(c) == topo.chip(me)]
        able = [c for c in onchip if all(topo.may_write(c, cores[d]) for d in cross)]
        plain = [c for c in onchip if c not in able and all(topo.may_write(c, cores[d]) for d in inpl)]
        pools = {}
        for x_plane, pool in ((True, able), (False, plain)):
            pools[(x_plane, True)] = [c for c in pool if topo.die(c) == topo.die(me)]
            pools[(x_plane, False)] = [c for c in pool if topo.die(c) != topo.die(me)]
        left = {True: list(cross), False: inpl[N_OWN:]}
        helpers = []
        for x_plane, same_die, cnt in HELPERS:
            c = pools[(x_plane, same_die)].pop(0)
            helpers.append((c, left[x_plane][:cnt]))
            left[x_plane] = left[x_plane][cnt:]
        plan.append({"direct": inpl[:N_OWN], "helpers": helpers})
    return plan


def _send(g, T, topo, core, dests, src, dst, bits, sem, local_sem):
    ids = []
    for d in dests:
        rid, pid = topo.addr(d, core)
        ids.append(DstId(rid=rid, pnc=pid))
    g.remote_dma_fused([RemoteDMATransfer(dst_ids=ids, dma_engine_mask=_mask(bits), remote_sem=sem,
                                          srcs=[src], dsts=[dst] * len(dests), alu_op=0)], local_sem=local_sem)


def rank_program(g, core, T, topo):
    cores = list(T.cores)
    plan = _plan(cores, topo)
    rank = T.rank_of(core)

    if rank is None:
        for j, pl in enumerate(plan):
            for c, dests in pl["helpers"]:
                if c == core:
                    bits = _bits(topo.mask(core, cores[dests[0]]))[:N_OFF]
                    g.wait_ge(T.sem["arr%d" % j], N_ON)
                    _send(g, T, topo, core, [cores[d] for d in dests], T.xd[:], T.xg[:, j * TK:(j + 1) * TK], bits,
                          T.sem["arr%d" % j], T.sem.sent)
                    g.wait_ge(T.sem.sent, N_OFF)
        return

    pl = plan[rank]
    coef = T.tables["COEF"][rank]
    av = [T.av[:, k * M:(k + 1) * M] for k in range(len(SCALES))]
    slot = T.xg[:, rank * TK:(rank + 1) * TK]
    arr = T.sem["arr%d" % rank]

    g.sync.dma_start(T.xd[:], T.x[:]).then_inc(T.sem.ldd, 16)
    g.sync.dma_start(av[0], T.a[:]).then_inc(T.sem.lda, 16)
    g.sync.wait_ge(T.sem.gone, N_ON)
    g.sync.dma_start(slot, T.x[:]).then_inc(T.sem.ldx, 16)

    off = _bits(topo.mask(core, cores[pl["direct"][0]]))
    on_only = [b for b in _bits(topo.mask(core, pl["helpers"][0][0])) if b not in off]
    g.wait_ge(T.sem.ldd, 16)
    _send(g, T, topo, core, [c for c, _ in pl["helpers"]], T.xd[:], T.xd[:], on_only[:N_ON], arr, T.sem.gone)
    _send(g, T, topo, core, [cores[d] for d in pl["direct"]], T.xd[:], slot, off[:N_OFF], arr, T.sem.sent)

    v = g.vector
    v.wait_ge(T.sem.lda, 16)
    v.tensor_tensor(av[1], av[0], av[0], AluOpType.add).then_inc(T.sem.sc, 1)
    v.wait_ge(T.sem.sc, 1)
    v.tensor_tensor(av[2], av[0], av[1], AluOpType.subtract).then_inc(T.sem.sc, 1)
    v.tensor_tensor(av[3], av[1], av[0], AluOpType.add).then_inc(T.sem.sc, 1)
    v.wait_ge(T.sem.sc, 3)
    v.tensor_tensor(av[4], av[2], av[0], AluOpType.subtract).then_inc(T.sem.sc, 1)

    due = [(3.5, rank, T.sem.ldx, 16)]
    for j, p in enumerate(plan):
        if rank in p["direct"]:
            due.append((p["direct"].index(rank) + 1.0, j, T.sem["arr%d" % j], N_OFF))
        for k, (c, dests) in enumerate(p["helpers"]):
            if rank in dests:
                due.append((1.4 + 0.4 * (k + 1) + dests.index(rank) + 1.0, j, T.sem["arr%d" % j], N_OFF))
    due.sort(key=lambda t: (t[0], t[1]))
    te = g.tensor
    te.wait_ge(T.sem.sc, 4)
    H = TK // 2
    for i, (_, j, sem, cnt) in enumerate(due):
        te.wait_ge(sem, cnt)
        lhs = av[SCALES.index(coef[j])]
        m0 = te.matmul(T.acc0[:, 0:H], lhs, T.xg[:, j * TK:j * TK + H], start=(i == 0), stop=(i == N - 1))
        m1 = te.matmul(T.acc1[:, 0:H], lhs, T.xg[:, j * TK + H:(j + 1) * TK], start=(i == 0), stop=(i == N - 1))
    m0.then_inc(T.sem.mm0, 1)
    m1.then_inc(T.sem.mm1, 1)

    v.wait_ge(T.sem.mm0, 1)
    v.tensor_copy(T.ys[:, 0:H], T.acc0[:, 0:H]).then_inc(T.sem.cp, 1)
    v.wait_ge(T.sem.mm1, 1)
    v.tensor_copy(T.ys[:, H:TK], T.acc1[:, 0:H]).then_inc(T.sem.cp, 1)
    g.sync.wait_ge(T.sem.cp, 2)
    g.sync.dma_start(T.y[:], T.ys[:]).then_inc(T.sem.st, 16)
    g.sync.wait_ge(T.sem.st, 16)
    g.wait_ge(T.sem.sent, N_OFF)
